import numpy as np
import ml_dtypes


def mxq(x, axis, fmt="e4m3"):
    dtype, down = {"e4m3": (ml_dtypes.float8_e4m3fn, 7), "e5m2": (ml_dtypes.float8_e5m2, 14)}[fmt]
    v = np.moveaxis(np.asarray(x, np.float32).astype(ml_dtypes.bfloat16).astype(np.float64), axis, -1)
    blocks = v.reshape(v.shape[:-1] + (-1, 32))
    amax = np.abs(blocks).max(-1, keepdims=True)
    byte = np.maximum(np.where(amax > 0, np.frexp(amax)[1] - 1 + 127, 0) - down, 1)
    scale = np.exp2(byte - 127.0)
    codes = (blocks / scale).astype(np.float32).astype(dtype).astype(np.float64)
    return np.moveaxis((codes * scale).reshape(v.shape), -1, axis)


WIDE = False


def mx_kscale(k):
    if not WIDE:
        return np.ones(k)
    levels = np.array([10, -10, 5, -5, 0])
    if k % 512:
        return np.exp2(np.random.permutation(np.resize(levels, k // 32))).repeat(32)
    a = np.empty((k // 512, 16))
    for p in range(k // 512):
        a[p, :8] = np.random.permutation(np.resize(levels, 8))
        for g in range(8):
            far = levels[np.abs(levels - a[p, g]) >= 10]
            a[p, g + 8] = far[np.random.randint(len(far))]
    return np.exp2(a.ravel()).repeat(32)


BF16 = ml_dtypes.bfloat16


def bf(x):
    return np.asarray(x, np.float32).astype(BF16)


def f64(x):
    return np.asarray(x).astype(np.float64)


E2M1 = np.array([0.0, 0.5, 1.0, 1.5, 2.0, 3.0, 4.0, 6.0, -0.0, -0.5, -1.0, -1.5, -2.0, -3.0, -4.0, -6.0])


def pack_weight(w, fmt):
    k, n = w.shape
    w = f64(bf(w)).reshape(k // 32, 32, n)
    amax = np.abs(w).max(1)
    if fmt == "e4m3":
        byte = np.frexp(amax)[1] - 1 + 127 - 7
    else:
        mant, ex = np.frexp(amax / 6.0)
        byte = np.where(mant > 0.5, ex, ex - 1) + 127
    byte = np.clip(np.where(amax > 0, byte, 1), 1, 254)
    scaled = (w * np.exp2(127.0 - byte)[:, None, :]).reshape(k, n).astype(np.float32)
    by_word = np.ascontiguousarray(scaled.reshape(k // 512, 128, 4, n).transpose(0, 1, 3, 2))
    if fmt == "e4m3":
        words = by_word.astype(ml_dtypes.float8_e4m3fn).view(np.uint8)
    else:
        c = by_word.astype(ml_dtypes.float4_e2m1fn).view(np.uint8) & 0xF
        words = c[..., 0::2] | (c[..., 1::2] << 4)
    return np.ascontiguousarray(words), np.ascontiguousarray(byte.astype(np.uint8).reshape(k // 512, 16, n))


def unpack_weight(words, scales, fmt):
    g, p, n, _ = words.shape
    if fmt == "e4m3":
        vals = np.ascontiguousarray(words).view(ml_dtypes.float8_e4m3fn).astype(np.float64)
    else:
        nib = np.empty((g, p, n, 4), np.uint8)
        nib[..., 0::2] = words & 0xF
        nib[..., 1::2] = words >> 4
        vals = E2M1[nib]
    vals = vals * np.repeat(np.exp2(scales.astype(np.float64) - 127.0), 8, axis=1)[..., None]
    return vals.transpose(0, 1, 3, 2).reshape(g * 512, n)


T, D, F, E, R = 1024, 1024, 1024, 128, 512


def softmax_last(l):
    m = np.max(l, axis=-1, keepdims=True)
    p = np.exp(l - m)
    return p / np.sum(p, axis=-1, keepdims=True)


def draw0():
    s, t = mx_kscale(D), mx_kscale(R)
    sd, sr = np.sqrt(D), np.sqrt(R)
    x = bf(np.random.standard_normal((T, D)) * s)
    w0_words, w0_scales = pack_weight(np.random.standard_normal((D, F)) / sd / s[:, None], "e4m3")
    wr_words, wr_scales = pack_weight(np.random.standard_normal((D, E)) / sd / s[:, None], "e4m3")
    br = bf(np.random.standard_normal(E) * 0.5)
    a_words, a_scales = pack_weight(np.random.standard_normal((D, R)) / sd / s[:, None] * t, "e4m3")
    b_words, b_scales = pack_weight(np.random.standard_normal((R, F)) * 0.6 / sr / t[:, None], "e4m3")
    return {
        "x": x,
        "w0_words": w0_words,
        "w0_scales": w0_scales,
        "wr_words": wr_words,
        "wr_scales": wr_scales,
        "br": br,
        "a_words": a_words,
        "a_scales": a_scales,
        "b_words": b_words,
        "b_scales": b_scales,
    }


def core(x, w0_words, w0_scales, wr_words, wr_scales, br, a_words, a_scales, b_words, b_scales):
    w0 = unpack_weight(w0_words, w0_scales, "e4m3")
    wr = unpack_weight(wr_words, wr_scales, "e4m3")
    a = unpack_weight(a_words, a_scales, "e4m3")
    b = unpack_weight(b_words, b_scales, "e4m3")
    n_tok = x.shape[0]
    n_exp = wr.shape[1]
    rank = a.shape[1]
    per_exp = rank // n_exp
    xq = mxq(f64(x), 1, "e4m3")
    l = (xq @ wr) + f64(br)
    g = float(n_exp) * softmax_last(l)
    u = xq @ a
    z = u.reshape(n_tok, n_exp, per_exp) * g[:, :, None]
    z = z.reshape(n_tok, rank)
    y = (xq @ w0) + (mxq(z, 1, "e4m3") @ b)
    return y


def e4m3fn_bytes(y):
    return np.clip(np.asarray(y, np.float64), -448.0, 448.0).astype(np.float32).astype(ml_dtypes.float8_e4m3fn).view(np.uint8)


def e4m3fn_values(b):
    return np.asarray(b, np.uint8).view(ml_dtypes.float8_e4m3fn).astype(np.float64)


def setup_inputs():
    d = draw0()
    x0 = np.asarray(d['x']).astype(np.float64)
    s = (np.max(np.abs(x0), axis=(0,), keepdims=True) / 448.0).astype(np.float32)
    out = {}
    for k, v in d.items():
        if k == 'x':
            out['x_bytes'] = e4m3fn_bytes(x0 / s.astype(np.float64))
            out['x_scale'] = s
        else:
            out[k] = v
    return out


def reference(x_bytes, x_scale, w0_words, w0_scales, wr_words, wr_scales, br, a_words, a_scales, b_words, b_scales):
    return core(e4m3fn_values(x_bytes) * x_scale.astype(np.float64), w0_words, w0_scales, wr_words, wr_scales, br, a_words, a_scales, b_words, b_scales)

@@ -1,0 +1,246 @@
+from contextlib import ExitStack
+
+import concourse.mybir as mybir
+from concourse.masks import make_identity
+
+T, D, F, E, R = 1024, 1024, 1024, 128, 512
+P = 128
+NT = T // P
+NXT, NLZ, NU, NO = 2, 2, 1, 3
+G = D // 512
+
+FLOPS = 2 * T * D * (F + E + R) + 2 * T * R * F
+
+F32 = mybir.dt.float32
+BF16 = mybir.dt.bfloat16
+I32 = mybir.dt.int32
+U32 = mybir.dt.uint32
+U8 = mybir.dt.uint8
+FP8 = mybir.dt.float8_e4m3fn
+FP8X4 = mybir.dt.float8_e4m3fn_x4
+ALU = mybir.AluOpType
+ACTF = mybir.ActivationFunctionType
+AX = mybir.AxisListType
+
+
+def tile_rankwisemoloradenserouter_w8_kernel(
+    tc, x_bytes, x_scale, w0_words, w0_scales, wr_words, wr_scales, br, a_words, a_scales, b_words, b_scales, out
+):
+    nc = tc.nc
+    with ExitStack() as ctx:
+        keep = ctx.enter_context(tc.tile_pool(name="keep", bufs=1))
+        work = ctx.enter_context(tc.tile_pool(name="work", bufs=3))
+        psum = ctx.enter_context(tc.psum_pool(name="psum", bufs=1))
+        ctx.enter_context(tc.manual_schedule())
+
+        ident = keep.tile([P, P], F32, name="ident", align_bytes=64)
+        xb = keep.tile([P, NT, D], U8, name="xb", align_bytes=64)
+        xs = keep.tile([P, G, 4], F32, name="xs", align_bytes=64)
+        brb = keep.tile([P, E], BF16, name="brb", align_bytes=64)
+        w0c = keep.tile([P, G, F], U32, name="w0c", align_bytes=64)
+        wrc = keep.tile([P, G, E], U32, name="wrc", align_bytes=64)
+        ac = keep.tile([P, G, R], U32, name="ac", align_bytes=64)
+        bc = keep.tile([P, F], U32, name="bc", align_bytes=64)
+        w0s = keep.tile([P, F], U8, name="w0s", align_bytes=64)
+        wrs = keep.tile([P, E], U8, name="wrs", align_bytes=64)
+        as_ = keep.tile([P, R], U8, name="as_", align_bytes=64)
+        bs = keep.tile([P, F], U8, name="bs", align_bytes=64)
+        warm = keep.tile([P, 1], F32, name="warm", align_bytes=64)
+
+        xv = x_bytes.rearrange("(p i) k -> p i k", i=NT)
+        ov = out.rearrange("(p i) f -> p i f", i=NT)
+
+        def load_words(dst, src):
+            nc.sync.dma_start(out=dst.bitcast(I32), in_=src.bitcast(I32))
+
+        def load_scales(dst, src, g):
+            for q in range(4):
+                nc.sync.dma_start(
+                    out=dst[32 * q : 32 * q + 4 * g, :].bitcast(I32),
+                    in_=src[:, 4 * q : 4 * q + 4, :].bitcast(I32),
+                )
+
+        nc.vector.memset(as_[:].bitcast(I32), 0)
+        nc.vector.memset(wrs[:].bitcast(I32), 0)
+        nc.vector.memset(warm[:], 0.0)
+        nc.vector.memset(w0s[:].bitcast(I32), 0)
+        nc.vector.memset(bs[:].bitcast(I32), 0)
+        make_identity(nc, ident[:])
+        nc.scalar.activation(out=warm[:], in_=warm[:], func=ACTF.Exp)
+
+        nc.sync.dma_start(out=xb[:, 0:2, :], in_=xv[:, 0:2, :])
+        nc.gpsimd.dma_start(out=xs[:], in_=x_scale.rearrange("o (g p t) -> p (o g) t", p=P, t=4))
+        nc.gpsimd.dma_start(out=brb[:], in_=br.partition_broadcast(P))
+        load_scales(as_, a_scales, G)
+        load_scales(wrs, wr_scales, G)
+        load_words(wrc[:], wr_words.rearrange("g p n t -> p g (n t)"))
+        load_words(ac[:], a_words.rearrange("g p n t -> p g (n t)"))
+        nc.sync.dma_start(out=xb[:, 2:4, :], in_=xv[:, 2:4, :])
+        load_scales(w0s, w0_scales, G)
+        load_words(w0c[:], w0_words.rearrange("g p n t -> p g (n t)"))
+        nc.sync.dma_start(out=xb[:, 4:8, :], in_=xv[:, 4:8, :])
+        load_scales(bs, b_scales, 1)
+        load_words(bc[:], b_words.rearrange("g p n t -> p g (n t)")[:, 0, :])
+
+        S = [dict() for i in range(NT)]
+
+        def W(i):
+            t = work.tile([P, D], BF16, name="xw", align_bytes=64)
+            src = xb[:, i, :].bitcast(FP8)
+            if i == 0:
+                nc.vector.tensor_copy(out=t[:, 0:512], in_=src[:, 0:512])
+                nc.scalar.copy(out=t[:, 512:1024], in_=src[:, 512:1024])
+            else:
+                nc.scalar.copy(out=t[:], in_=src)
+            S[i]["xw"] = t
+
+        def TR(i):
+            t = psum.tile([P, G, 2, P], F32, name="xt", bufs=NXT)
+            words = S[i]["xw"][:].bitcast(F32)
+            for g in range(G):
+                for u in range(2):
+                    nc.tensor.transpose(t[:, g, u, :], words[:, 256 * g + u : 256 * (g + 1) : 2], ident[:])
+            S[i]["xt"] = t
+
+        def M(i, g):
+            if g == 0:
+                S[i]["xg"] = work.tile([P, G, P, 4], BF16, name="xg", align_bytes=64)
+            src = S[i]["xt"][:, g, :, :].rearrange("p u n -> p (u n)").bitcast(BF16)
+            nc.vector.tensor_tensor(
+                out=S[i]["xg"][:, g, :, :].rearrange("p n (u e) -> p n u e", e=2),
+                in0=src.rearrange("p (u n e) -> p n u e", u=2, e=2),
+                in1=xs[:, g, :].rearrange("p (u e) -> p u e", e=2).unsqueeze(1).to_broadcast([P, P, 2, 2]),
+                op=ALU.mult,
+            )
+
+        def Q(i):
+            c = keep.tile([P, G, P], U32, name="xc%d" % i, align_bytes=64)
+            s = keep.tile([P, G, P], U8, name="xcs%d" % i, align_bytes=64)
+            nc.vector.quantize_mx(
+                out=c[:].rearrange("p g n -> p (g n)").bitcast(FP8X4),
+                scales=s[:].rearrange("p g n -> p (g n)"),
+                in_=S[i]["xg"][:].rearrange("p g n t -> p (g n t)"),
+            )
+            S[i]["xc"], S[i]["xcs"] = c, s
+
+        def mm(dst, i, g, wc, ws, cols, start, stop):
+            nc.tensor.matmul_mx(
+                out=dst,
+                lhsT=S[i]["xc"][:, g, :].bitcast(FP8X4),
+                lhsT_scale=S[i]["xcs"][:, g, :],
+                rhs=wc[:, g, cols].bitcast(FP8X4),
+                rhs_scale=ws[4 * g : P, cols],
+                start=start,
+                stop=stop,
+            )
+
+        def L(i):
+            l = psum.tile([P, E], F32, name="lz", bufs=NLZ)
+            for g in range(G):
+                mm(l[:], i, g, wrc, wrs, slice(0, E), g == 0, g == G - 1)
+            S[i]["l"] = l
+
+        def U(i):
+            u = psum.tile([P, R], F32, name="u", bufs=NU)
+            for g in range(G):
+                mm(u[:], i, g, ac, as_, slice(0, R), g == 0, g == G - 1)
+            S[i]["u"] = u
+
+        def A(i):
+            lb = work.tile([P, E], F32, name="lb", align_bytes=64)
+            nm = work.tile([P, 1], F32, name="nm", align_bytes=64)
+            nc.vector.tensor_tensor(out=lb[:], in0=S[i]["l"][:], in1=brb[:], op=ALU.add)
+            nc.vector.tensor_reduce(out=nm[:], in_=lb[:], axis=AX.X, op=ALU.max, negate=True)
+            S[i]["lb"], S[i]["nm"] = lb, nm
+
+        def X(i):
+            ex = work.tile([P, E], F32, name="ex", align_bytes=64)
+            sm = work.tile([P, 1], F32, name="sm", align_bytes=64)
+            nc.scalar.activation(out=ex[:], in_=S[i]["lb"][:], func=ACTF.Exp, bias=S[i]["nm"][:], scale=1.0, accum_out=sm[:])
+            S[i]["ex"], S[i]["sm"] = ex, sm
+
+        def RC(i):
+            r0 = work.tile([P, 1], F32, name="r0", align_bytes=64)
+            r1 = work.tile([P, 1], F32, name="r1", align_bytes=64)
+            nc.vector.reciprocal(out=r0[:], in_=S[i]["sm"][:])
+            nc.vector.tensor_scalar(out=r1[:], in0=r0[:], scalar1=float(E), scalar2=None, op0=ALU.mult)
+            S[i]["r"] = r1
+
+        def Z(i):
+            z = work.tile([P, 2, E, 2], BF16, name="z", align_bytes=64)
+            uv = S[i]["u"][:].rearrange("p (m u e) -> p u m e", u=2, e=2)
+            exv = S[i]["ex"][:].unsqueeze(2).to_broadcast([P, E, 2])
+            for u in range(2):
+                nc.vector.scalar_tensor_tensor(
+                    out=z[:, u, :, :], in0=uv[:, u, :, :], scalar=S[i]["r"][:], in1=exv, op0=ALU.mult, op1=ALU.mult
+                )
+            S[i]["z"] = z
+
+        def ZT(i):
+            t = psum.tile([P, 2, P], F32, name="lz", bufs=NLZ)
+            words = S[i]["z"][:].rearrange("p u m e -> p (u m e)").bitcast(F32)
+            for u in range(2):
+                nc.tensor.transpose(t[:, u, :], words[:, P * u : P * (u + 1)], ident[:])
+            S[i]["zt"] = t
+
+        def ZE(i):
+            t = work.tile([P, P, 4], BF16, name="zg", align_bytes=64)
+            nc.scalar.copy(
+                out=t[:].rearrange("p n t -> p (n t)").bitcast(F32).rearrange("p (n u) -> p n u", u=2),
+                in_=S[i]["zt"][:].rearrange("p u n -> p n u"),
+            )
+            S[i]["zg"] = t
+
+        def ZQ(i):
+            c = work.tile([P, P], U32, name="zc", align_bytes=64)
+            s = work.tile([P, P], U8, name="zcs", align_bytes=64)
+            nc.vector.quantize_mx(out=c[:].bitcast(FP8X4), scales=s[:], in_=S[i]["zg"][:].rearrange("p n t -> p (n t)"))
+            S[i]["zc"], S[i]["zcs"] = c, s
+
+        def B(i, h):
+            o = psum.tile([P, 512], F32, name="o", bufs=NO)
+            for g in range(G):
+                mm(o[:], i, g, w0c, w0s, slice(512 * h, 512 * h + 512), g == 0, False)
+            S[i]["o%d" % h] = o
+
+        def C(i, h):
+            cols = slice(512 * h, 512 * h + 512)
+            nc.tensor.matmul_mx(
+                out=S[i]["o%d" % h][:],
+                lhsT=S[i]["zc"][:].bitcast(FP8X4),
+                lhsT_scale=S[i]["zcs"][:],
+                rhs=bc[:, cols].bitcast(FP8X4),
+                rhs_scale=bs[:, cols],
+                start=False,
+                stop=True,
+            )
+
+        def EV(i, h):
+            t = work.tile([P, 512], F32, name="ot", bufs=4, align_bytes=64)
+            nc.scalar.copy(out=t[:], in_=S[i]["o%d" % h][:])
+            nc.sync.dma_start(out=ov[:, i, 512 * h : 512 * h + 512], in_=t[:])
+
+        stages = [
+            (-14.690, lambda i: W(i)),
+            (-13.540, lambda i: TR(i)),
+            (-12.570, lambda i: M(i, 0)),
+            (-11.890, lambda i: M(i, 1)),
+            (-11.760, lambda i: Q(i)),
+            (-11.570, lambda i: L(i)),
+            (-11.530, lambda i: A(i)),
+            (-11.240, lambda i: X(i)),
+            (-11.170, lambda i: U(i)),
+            (-10.880, lambda i: RC(i)),
+            (-10.620, lambda i: B(i, 0)),
+            (-10.610, lambda i: Z(i)),
+            (-10.500, lambda i: ZT(i)),
+            (-10.250, lambda i: ZE(i)),
+            (-9.990, lambda i: B(i, 1)),
+            (-9.880, lambda i: ZQ(i)),
+            (-9.710, lambda i: C(i, 0)),
+            (-9.470, lambda i: C(i, 1)),
+            (-9.370, lambda i: EV(i, 0)),
+            (-9.170, lambda i: EV(i, 1)),
+        ]
+        for when, k, i in sorted((i + ph, k, i) for k, (ph, f) in enumerate(stages) for i in range(NT)):
+            stages[k][1](i)

@@ -6,8 +6,8 @@ from concourse.masks import make_identity
 T, D, F, E, R = 1024, 1024, 1024, 128, 512
 P = 128
 NT = T // P
-NXT, NLZ, NU, NO = 2, 2, 1, 3
 G = D // 512
+NXT, NLZ, NU, NO, NWORK, NWV, ND1, ND2 = 2, 1, 2, 3, 8, 2, 3, 2
 
 FLOPS = 2 * T * D * (F + E + R) + 2 * T * R * F
 
@@ -29,7 +29,7 @@ def tile_rankwisemoloradenserouter_w8_kernel(
     nc = tc.nc
     with ExitStack() as ctx:
         keep = ctx.enter_context(tc.tile_pool(name="keep", bufs=1))
-        work = ctx.enter_context(tc.tile_pool(name="work", bufs=3))
+        work = ctx.enter_context(tc.tile_pool(name="work", bufs=NWORK))
         psum = ctx.enter_context(tc.psum_pool(name="psum", bufs=1))
         ctx.enter_context(tc.manual_schedule())
 
@@ -46,6 +46,7 @@ def tile_rankwisemoloradenserouter_w8_kernel(
         as_ = keep.tile([P, R], U8, name="as_", align_bytes=64)
         bs = keep.tile([P, F], U8, name="bs", align_bytes=64)
         warm = keep.tile([P, 1], F32, name="warm", align_bytes=64)
+        dmy = keep.tile([P, 512], BF16, name="dmy", align_bytes=64)
 
         xv = x_bytes.rearrange("(p i) k -> p i k", i=NT)
         ov = out.rearrange("(p i) f -> p i f", i=NT)
@@ -60,52 +61,68 @@ def tile_rankwisemoloradenserouter_w8_kernel(
                     in_=src[:, 4 * q : 4 * q + 4, :].bitcast(I32),
                 )
 
-        nc.vector.memset(as_[:].bitcast(I32), 0)
         nc.vector.memset(wrs[:].bitcast(I32), 0)
-        nc.vector.memset(warm[:], 0.0)
+        nc.vector.memset(as_[:].bitcast(I32), 0)
         nc.vector.memset(w0s[:].bitcast(I32), 0)
+        nc.vector.memset(dmy[:].bitcast(I32), 0)
+        nc.vector.memset(warm[:], 0.0)
         nc.vector.memset(bs[:].bitcast(I32), 0)
         make_identity(nc, ident[:])
-        nc.scalar.activation(out=warm[:], in_=warm[:], func=ACTF.Exp)
 
-        nc.sync.dma_start(out=xb[:, 0:2, :], in_=xv[:, 0:2, :])
-        nc.gpsimd.dma_start(out=xs[:], in_=x_scale.rearrange("o (g p t) -> p (o g) t", p=P, t=4))
-        nc.gpsimd.dma_start(out=brb[:], in_=br.partition_broadcast(P))
-        load_scales(as_, a_scales, G)
+        nc.sync.dma_start(out=xb[:, 0, :], in_=xv[:, 0, :])
+        nc.scalar.dma_start(out=xs[:], in_=x_scale.rearrange("o (g p t) -> p (o g) t", p=P, t=4))
+        nc.scalar.activation(out=warm[:], in_=warm[:], func=ACTF.Exp)
+        nc.sync.dma_start(out=xb[:, 1, :], in_=xv[:, 1, :])
         load_scales(wrs, wr_scales, G)
         load_words(wrc[:], wr_words.rearrange("g p n t -> p g (n t)"))
-        load_words(ac[:], a_words.rearrange("g p n t -> p g (n t)"))
         nc.sync.dma_start(out=xb[:, 2:4, :], in_=xv[:, 2:4, :])
-        load_scales(w0s, w0_scales, G)
-        load_words(w0c[:], w0_words.rearrange("g p n t -> p g (n t)"))
+        load_words(ac[:], a_words.rearrange("g p n t -> p g (n t)"))
+        load_scales(as_, a_scales, G)
+        nc.sync.dma_start(out=brb[:], in_=br.partition_broadcast(P))
         nc.sync.dma_start(out=xb[:, 4:8, :], in_=xv[:, 4:8, :])
-        load_scales(bs, b_scales, 1)
+        load_words(w0c[:], w0_words.rearrange("g p n t -> p g (n t)"))
+        load_scales(w0s, w0_scales, G)
         load_words(bc[:], b_words.rearrange("g p n t -> p g (n t)")[:, 0, :])
+        load_scales(bs, b_scales, 1)
 
         S = [dict() for i in range(NT)]
 
+        def dummy(n):
+            for k in range(n):
+                t = psum.tile([P, 512], F32, name="u", bufs=NU)
+                nc.tensor.matmul(t[:], lhsT=dmy[:, 0:P], rhs=dmy[:], start=True, stop=True)
+
+        def xw(i):
+            if "xw" not in S[i]:
+                S[i]["xw"] = work.tile([P, D], BF16, name="xw", align_bytes=64)
+            return S[i]["xw"]
+
+        def WV(i):
+            eng = nc.vector if i < NWV else nc.gpsimd
+            eng.tensor_copy(out=xw(i)[:, 0:512], in_=xb[:, i, 0:512].bitcast(FP8))
+
         def W(i):
-            t = work.tile([P, D], BF16, name="xw", align_bytes=64)
-            src = xb[:, i, :].bitcast(FP8)
-            if i == 0:
-                nc.vector.tensor_copy(out=t[:, 0:512], in_=src[:, 0:512])
-                nc.scalar.copy(out=t[:, 512:1024], in_=src[:, 512:1024])
-            else:
-                nc.scalar.copy(out=t[:], in_=src)
-            S[i]["xw"] = t
+            nc.scalar.copy(out=xw(i)[:, 512:D], in_=xb[:, i, 512:D].bitcast(FP8))
+
 
         def TR(i):
-            t = psum.tile([P, G, 2, P], F32, name="xt", bufs=NXT)
             words = S[i]["xw"][:].bitcast(F32)
+            if i == 0:
+                parts = [psum.tile([P, 2, P], F32, name="xt", bufs=NXT) for g in range(G)]
+                S[i]["xt"] = [t[:, :, :] for t in parts]
+            else:
+                t = psum.tile([P, G, 2, P], F32, name="xt", bufs=NXT)
+                S[i]["xt"] = [t[:, g, :, :] for g in range(G)]
             for g in range(G):
                 for u in range(2):
-                    nc.tensor.transpose(t[:, g, u, :], words[:, 256 * g + u : 256 * (g + 1) : 2], ident[:])
-            S[i]["xt"] = t
+                    nc.tensor.transpose(S[i]["xt"][g][:, u, :], words[:, 256 * g + u : 256 * (g + 1) : 2], ident[:])
+            if i == 0:
+                dummy(ND2)
 
         def M(i, g):
             if g == 0:
                 S[i]["xg"] = work.tile([P, G, P, 4], BF16, name="xg", align_bytes=64)
-            src = S[i]["xt"][:, g, :, :].rearrange("p u n -> p (u n)").bitcast(BF16)
+            src = S[i]["xt"][g].rearrange("p u n -> p (u n)").bitcast(BF16)
             nc.vector.tensor_tensor(
                 out=S[i]["xg"][:, g, :, :].rearrange("p n (u e) -> p n u e", e=2),
                 in0=src.rearrange("p (u n e) -> p n u e", u=2, e=2),
@@ -113,15 +130,22 @@ def tile_rankwisemoloradenserouter_w8_kernel(
                 op=ALU.mult,
             )
 
-        def Q(i):
-            c = keep.tile([P, G, P], U32, name="xc%d" % i, align_bytes=64)
-            s = keep.tile([P, G, P], U8, name="xcs%d" % i, align_bytes=64)
+        def quant(i, gs):
+            if "xc" not in S[i]:
+                S[i]["xc"] = keep.tile([P, G, P], U32, name="xc%d" % i, align_bytes=64)
+                S[i]["xcs"] = keep.tile([P, G, P], U8, name="xcs%d" % i, align_bytes=64)
             nc.vector.quantize_mx(
-                out=c[:].rearrange("p g n -> p (g n)").bitcast(FP8X4),
-                scales=s[:].rearrange("p g n -> p (g n)"),
-                in_=S[i]["xg"][:].rearrange("p g n t -> p (g n t)"),
+                out=S[i]["xc"][:, gs, :].rearrange("p g n -> p (g n)").bitcast(FP8X4),
+                scales=S[i]["xcs"][:, gs, :].rearrange("p g n -> p (g n)"),
+                in_=S[i]["xg"][:, gs, :, :].rearrange("p g n t -> p (g n t)"),
             )
-            S[i]["xc"], S[i]["xcs"] = c, s
+
+        def Q(i):
+            quant(i, slice(0, 1) if i == 0 else slice(0, G))
+
+        def QB(i):
+            if i == 0:
+                quant(i, slice(1, 2))
 
         def mm(dst, i, g, wc, ws, cols, start, stop):
             nc.tensor.matmul_mx(
@@ -148,10 +172,13 @@ def tile_rankwisemoloradenserouter_w8_kernel(
 
         def A(i):
             lb = work.tile([P, E], F32, name="lb", align_bytes=64)
-            nm = work.tile([P, 1], F32, name="nm", align_bytes=64)
             nc.vector.tensor_tensor(out=lb[:], in0=S[i]["l"][:], in1=brb[:], op=ALU.add)
-            nc.vector.tensor_reduce(out=nm[:], in_=lb[:], axis=AX.X, op=ALU.max, negate=True)
-            S[i]["lb"], S[i]["nm"] = lb, nm
+            S[i]["lb"] = lb
+
+        def A2(i):
+            nm = work.tile([P, 1], F32, name="nm", align_bytes=64)
+            nc.vector.tensor_reduce(out=nm[:], in_=S[i]["lb"][:], axis=AX.X, op=ALU.max, negate=True)
+            S[i]["nm"] = nm
 
         def X(i):
             ex = work.tile([P, E], F32, name="ex", align_bytes=64)
@@ -159,22 +186,27 @@ def tile_rankwisemoloradenserouter_w8_kernel(
             nc.scalar.activation(out=ex[:], in_=S[i]["lb"][:], func=ACTF.Exp, bias=S[i]["nm"][:], scale=1.0, accum_out=sm[:])
             S[i]["ex"], S[i]["sm"] = ex, sm
 
-        def RC(i):
+        def R1(i):
             r0 = work.tile([P, 1], F32, name="r0", align_bytes=64)
-            r1 = work.tile([P, 1], F32, name="r1", align_bytes=64)
             nc.vector.reciprocal(out=r0[:], in_=S[i]["sm"][:])
-            nc.vector.tensor_scalar(out=r1[:], in0=r0[:], scalar1=float(E), scalar2=None, op0=ALU.mult)
+            S[i]["r0"] = r0
+
+        def R2(i):
+            r1 = work.tile([P, 1], F32, name="r1", align_bytes=64)
+            nc.vector.tensor_scalar(out=r1[:], in0=S[i]["r0"][:], scalar1=float(E), scalar2=None, op0=ALU.mult)
             S[i]["r"] = r1
 
-        def Z(i):
-            z = work.tile([P, 2, E, 2], BF16, name="z", align_bytes=64)
-            uv = S[i]["u"][:].rearrange("p (m u e) -> p u m e", u=2, e=2)
-            exv = S[i]["ex"][:].unsqueeze(2).to_broadcast([P, E, 2])
-            for u in range(2):
-                nc.vector.scalar_tensor_tensor(
-                    out=z[:, u, :, :], in0=uv[:, u, :, :], scalar=S[i]["r"][:], in1=exv, op0=ALU.mult, op1=ALU.mult
-                )
-            S[i]["z"] = z
+        def Z(i, u):
+            if u == 0:
+                S[i]["z"] = work.tile([P, 2, E, 2], BF16, name="z", align_bytes=64)
+            nc.vector.scalar_tensor_tensor(
+                out=S[i]["z"][:, u, :, :],
+                in0=S[i]["u"][:].rearrange("p (m u e) -> p u m e", u=2, e=2)[:, u, :, :],
+                scalar=S[i]["r"][:],
+                in1=S[i]["ex"][:].unsqueeze(2).to_broadcast([P, E, 2]),
+                op0=ALU.mult,
+                op1=ALU.mult,
+            )
 
         def ZT(i):
             t = psum.tile([P, 2, P], F32, name="lz", bufs=NLZ)
@@ -217,30 +249,203 @@ def tile_rankwisemoloradenserouter_w8_kernel(
 
         def EV(i, h):
             t = work.tile([P, 512], F32, name="ot", bufs=4, align_bytes=64)
-            nc.scalar.copy(out=t[:], in_=S[i]["o%d" % h][:])
+            if i == NT - 1 and h == 1:
+                nc.vector.tensor_copy(out=t[:], in_=S[i]["o%d" % h][:])
+            else:
+                nc.scalar.copy(out=t[:], in_=S[i]["o%d" % h][:])
             nc.sync.dma_start(out=ov[:, i, 512 * h : 512 * h + 512], in_=t[:])
 
-        stages = [
-            (-14.690, lambda i: W(i)),
-            (-13.540, lambda i: TR(i)),
-            (-12.570, lambda i: M(i, 0)),
-            (-11.890, lambda i: M(i, 1)),
-            (-11.760, lambda i: Q(i)),
-            (-11.570, lambda i: L(i)),
-            (-11.530, lambda i: A(i)),
-            (-11.240, lambda i: X(i)),
-            (-11.170, lambda i: U(i)),
-            (-10.880, lambda i: RC(i)),
-            (-10.620, lambda i: B(i, 0)),
-            (-10.610, lambda i: Z(i)),
-            (-10.500, lambda i: ZT(i)),
-            (-10.250, lambda i: ZE(i)),
-            (-9.990, lambda i: B(i, 1)),
-            (-9.880, lambda i: ZQ(i)),
-            (-9.710, lambda i: C(i, 0)),
-            (-9.470, lambda i: C(i, 1)),
-            (-9.370, lambda i: EV(i, 0)),
-            (-9.170, lambda i: EV(i, 1)),
-        ]
-        for when, k, i in sorted((i + ph, k, i) for k, (ph, f) in enumerate(stages) for i in range(NT)):
-            stages[k][1](i)
+        dummy(ND1)
+        WV(0)
+        W(0)
+        WV(1)
+        W(1)
+        TR(0)
+        W(2)
+        WV(2)
+        M(0, 0)
+        W(3)
+        WV(3)
+        Q(0)
+        TR(1)
+        M(0, 1)
+        M(1, 0)
+        TR(2)
+        QB(0)
+        W(4)
+        WV(4)
+        M(1, 1)
+        L(0)
+        W(5)
+        U(0)
+        WV(5)
+        M(2, 0)
+        W(6)
+        TR(3)
+        A(0)
+        WV(6)
+        Q(1)
+        W(7)
+        A2(0)
+        B(0, 1)
+        M(2, 1)
+        WV(7)
+        X(0)
+        L(1)
+        M(3, 0)
+        U(1)
+        A(1)
+        R1(0)
+        Q(2)
+        TR(4)
+        A2(1)
+        R2(0)
+        M(3, 1)
+        L(2)
+        X(1)
+        B(1, 1)
+        Z(0, 0)
+        A(2)
+        R1(1)
+        TR(5)
+        Q(3)
+        Z(0, 1)
+        A2(2)
+        L(3)
+        R2(1)
+        M(4, 0)
+        U(2)
+        X(2)
+        Z(1, 0)
+        B(0, 0)
+        A(3)
+        R1(2)
+        M(4, 1)
+        ZT(0)
+        Z(1, 1)
+        ZE(0)
+        A2(3)
+        TR(6)
+        R2(2)
+        Q(4)
+        X(3)
+        Z(2, 0)
+        ZT(1)
+        ZQ(0)
+        U(3)
+        M(5, 0)
+        ZE(1)
+        C(0, 0)
+        Z(2, 1)
+        L(4)
+        ZQ(1)
+        C(0, 1)
+        R1(3)
+        M(5, 1)
+        EV(0, 0)
+        U(4)
+        A(4)
+        EV(0, 1)
+        R2(3)
+        C(1, 1)
+        M(6, 0)
+        TR(7)
+        Z(3, 0)
+        EV(1, 1)
+        A2(4)
+        ZT(2)
+        Q(5)
+        B(2, 1)
+        Z(3, 1)
+        ZE(2)
+        M(6, 1)
+        X(4)
+        B(1, 0)
+        ZQ(2)
+        L(5)
+        R1(4)
+        M(7, 0)
+        C(1, 0)
+        U(5)
+        A(5)
+        EV(1, 0)
+        R2(4)
+        Q(6)
+        C(2, 1)
+        Z(4, 0)
+        ZT(3)
+        A2(5)
+        M(7, 1)
+        B(3, 1)
+        ZE(3)
+        X(5)
+        Z(4, 1)
+        B(2, 0)
+        EV(2, 1)
+        Q(7)
+        L(6)
+        ZQ(3)
+        C(2, 0)
+        R1(5)
+        U(6)
+        A(6)
+        R2(5)
+        EV(2, 0)
+        A2(6)
+        L(7)
+        Z(5, 0)
+        C(3, 1)
+        B(4, 1)
+        X(6)
+        A(7)
+        Z(5, 1)
+        EV(3, 1)
+        A2(7)
+        ZT(4)
+        R1(6)
+        U(7)
+        R2(6)
+        ZE(4)
+        X(7)
+        Z(6, 0)
+        B(3, 0)
+        ZQ(4)
+        R1(7)
+        Z(6, 1)
+        ZT(5)
+        R2(7)
+        C(3, 0)
+        ZE(5)
+        C(4, 1)
+        Z(7, 0)
+        B(5, 1)
+        EV(3, 0)
+        ZQ(5)
+        Z(7, 1)
+        EV(4, 1)
+        ZT(6)
+        C(5, 1)
+        ZE(6)
+        B(4, 0)
+        EV(5, 1)
+        C(4, 0)
+        ZQ(6)
+        ZT(7)
+        B(6, 1)
+        ZE(7)
+        EV(4, 0)
+        C(6, 1)
+        B(5, 0)
+        ZQ(7)
+        EV(6, 1)
+        C(5, 0)
+        B(7, 1)
+        EV(5, 0)
+        C(7, 1)
+        B(6, 0)
+        EV(7, 1)
+        C(6, 0)
+        B(7, 0)
+        EV(6, 0)
+        C(7, 0)
+        EV(7, 0)

@@ -7,7 +7,7 @@ T, D, F, E, R = 1024, 1024, 1024, 128, 512
 P = 128
 NT = T // P
 G = D // 512
-NXT, NLZ, NU, NO, NWORK, NWV, ND1, ND2 = 2, 1, 2, 3, 8, 2, 3, 2
+NXT, NLZ, NU, NO, NWORK, ND1, ND2, ZPERM, WG, NS = 2, 1, 2, 3, 8, 3, 2, True, True, 8
 
 FLOPS = 2 * T * D * (F + E + R) + 2 * T * R * F
 
@@ -73,9 +73,9 @@ def tile_rankwisemoloradenserouter_w8_kernel(
         nc.scalar.dma_start(out=xs[:], in_=x_scale.rearrange("o (g p t) -> p (o g) t", p=P, t=4))
         nc.scalar.activation(out=warm[:], in_=warm[:], func=ACTF.Exp)
         nc.sync.dma_start(out=xb[:, 1, :], in_=xv[:, 1, :])
-        load_scales(wrs, wr_scales, G)
-        load_words(wrc[:], wr_words.rearrange("g p n t -> p g (n t)"))
         nc.sync.dma_start(out=xb[:, 2:4, :], in_=xv[:, 2:4, :])
+        load_words(wrc[:], wr_words.rearrange("g p n t -> p g (n t)"))
+        load_scales(wrs, wr_scales, G)
         load_words(ac[:], a_words.rearrange("g p n t -> p g (n t)"))
         load_scales(as_, a_scales, G)
         nc.sync.dma_start(out=brb[:], in_=br.partition_broadcast(P))
@@ -92,142 +92,262 @@ def tile_rankwisemoloradenserouter_w8_kernel(
                 t = psum.tile([P, 512], F32, name="u", bufs=NU)
                 nc.tensor.matmul(t[:], lhsT=dmy[:, 0:P], rhs=dmy[:], start=True, stop=True)
 
-        def xw(i):
+        def fp8(i, k0, k1):
+            return xb[:, i, k0:k1].bitcast(FP8)
+
+        def newx(i):
             if "xw" not in S[i]:
                 S[i]["xw"] = work.tile([P, D], BF16, name="xw", align_bytes=64)
             return S[i]["xw"]
 
-        def WV(i):
-            eng = nc.vector if i < NWV else nc.gpsimd
-            eng.tensor_copy(out=xw(i)[:, 0:512], in_=xb[:, i, 0:512].bitcast(FP8))
+        def wv(i):
+            if i < 2:
+                nc.vector.tensor_copy(out=newx(i)[:, 0:512], in_=fp8(i, 0, 512))
+            elif WG:
+                for k in (0, 256):
+                    nc.gpsimd.tensor_copy(out=newx(i)[:, k : k + 256], in_=fp8(i, k, k + 256))
 
-        def W(i):
-            nc.scalar.copy(out=xw(i)[:, 512:D], in_=xb[:, i, 512:D].bitcast(FP8))
+        def w(i):
+            k = 512 if i < 2 or WG else 0
+            nc.scalar.copy(out=newx(i)[:, k:D], in_=fp8(i, k, D))
 
+        def Wa(i):
+            nc.scalar.copy(out=newx(i)[:], in_=fp8(i, 0, D))
 
-        def TR(i):
+        def Wb(i):
+            for k in range(4):
+                nc.gpsimd.tensor_copy(out=newx(i + 1)[:, 256 * k : 256 * (k + 1)], in_=fp8(i + 1, 256 * k, 256 * (k + 1)))
+
+        def turn(dst, i, g):
             words = S[i]["xw"][:].bitcast(F32)
+            for u in range(2):
+                nc.tensor.transpose(dst[u], words[:, 256 * g + u : 256 * (g + 1) : 2], ident[:])
+
+        def t(i):
             if i == 0:
-                parts = [psum.tile([P, 2, P], F32, name="xt", bufs=NXT) for g in range(G)]
-                S[i]["xt"] = [t[:, :, :] for t in parts]
+                S[i]["xt"] = [psum.tile([P, 2, P], F32, name="xt", bufs=NXT)[:, :, :] for g in range(G)]
             else:
-                t = psum.tile([P, G, 2, P], F32, name="xt", bufs=NXT)
-                S[i]["xt"] = [t[:, g, :, :] for g in range(G)]
+                x1 = psum.tile([P, G, 2, P], F32, name="xt", bufs=NXT)
+                S[i]["xt"] = [x1[:, g, :, :] for g in range(G)]
             for g in range(G):
-                for u in range(2):
-                    nc.tensor.transpose(S[i]["xt"][g][:, u, :], words[:, 256 * g + u : 256 * (g + 1) : 2], ident[:])
+                turn([S[i]["xt"][g][:, u, :] for u in range(2)], i, g)
             if i == 0:
                 dummy(ND2)
 
-        def M(i, g):
-            if g == 0:
-                S[i]["xg"] = work.tile([P, G, P, 4], BF16, name="xg", align_bytes=64)
-            src = S[i]["xt"][g].rearrange("p u n -> p (u n)").bitcast(BF16)
+        def T(i, g):
+            xp = psum.tile([P, 2, 2, P], F32, name="xt", bufs=NXT)
+            for k in range(2):
+                turn([xp[:, u, k, :] for u in range(2)], i + k, g)
+            S[i]["xt%d" % g] = xp[:].rearrange("p u k n -> p u (k n)")
+
+        def scale(i, g, n, src):
+            if "xg" not in S[i]:
+                S[i]["xg"] = work.tile([P, G, n * P, 4], BF16, name="xg%d" % n, align_bytes=64)
             nc.vector.tensor_tensor(
                 out=S[i]["xg"][:, g, :, :].rearrange("p n (u e) -> p n u e", e=2),
-                in0=src.rearrange("p (u n e) -> p n u e", u=2, e=2),
-                in1=xs[:, g, :].rearrange("p (u e) -> p u e", e=2).unsqueeze(1).to_broadcast([P, P, 2, 2]),
+                in0=src.rearrange("p u n -> p (u n)").bitcast(BF16).rearrange("p (u n e) -> p n u e", u=2, e=2),
+                in1=xs[:, g, :].rearrange("p (u e) -> p u e", e=2).unsqueeze(1).to_broadcast([P, n * P, 2, 2]),
                 op=ALU.mult,
             )
 
-        def quant(i, gs):
+        def ma(i):
+            scale(i, 0, 1, S[i]["xt"][0])
+
+        def mb(i):
+            scale(i, 1, 1, S[i]["xt"][1])
+
+        def M(i, g):
+            scale(i, g, 2, S[i]["xt%d" % g])
+
+        def quant(i, n, gs):
             if "xc" not in S[i]:
-                S[i]["xc"] = keep.tile([P, G, P], U32, name="xc%d" % i, align_bytes=64)
-                S[i]["xcs"] = keep.tile([P, G, P], U8, name="xcs%d" % i, align_bytes=64)
+                S[i]["xc"] = keep.tile([P, G, n * P], U32, name="xc%d" % i, align_bytes=64)
+                S[i]["xcs"] = keep.tile([P, G, n * P], U8, name="xcs%d" % i, align_bytes=64)
+                for k in range(n):
+                    S[i + k]["x"] = (S[i]["xc"], S[i]["xcs"], slice(k * P, (k + 1) * P))
             nc.vector.quantize_mx(
                 out=S[i]["xc"][:, gs, :].rearrange("p g n -> p (g n)").bitcast(FP8X4),
                 scales=S[i]["xcs"][:, gs, :].rearrange("p g n -> p (g n)"),
                 in_=S[i]["xg"][:, gs, :, :].rearrange("p g n t -> p (g n t)"),
             )
 
-        def Q(i):
-            quant(i, slice(0, 1) if i == 0 else slice(0, G))
+        def q(i):
+            quant(i, 1, slice(0, 1) if i == 0 else slice(0, G))
 
-        def QB(i):
-            if i == 0:
-                quant(i, slice(1, 2))
+        def qb(i):
+            quant(i, 1, slice(1, G))
+
+        def Q(i):
+            quant(i, 2, slice(0, G))
 
         def mm(dst, i, g, wc, ws, cols, start, stop):
+            c, s, tok = S[i]["x"]
             nc.tensor.matmul_mx(
                 out=dst,
-                lhsT=S[i]["xc"][:, g, :].bitcast(FP8X4),
-                lhsT_scale=S[i]["xcs"][:, g, :],
+                lhsT=c[:, g, tok].bitcast(FP8X4),
+                lhsT_scale=s[:, g, tok],
                 rhs=wc[:, g, cols].bitcast(FP8X4),
                 rhs_scale=ws[4 * g : P, cols],
                 start=start,
                 stop=stop,
             )
 
-        def L(i):
-            l = psum.tile([P, E], F32, name="lz", bufs=NLZ)
-            for g in range(G):
-                mm(l[:], i, g, wrc, wrs, slice(0, E), g == 0, g == G - 1)
+        def logits(i, n):
+            l = psum.tile([P, n, E], F32, name="lz", bufs=NLZ)
+            for k in range(n):
+                for g in range(G):
+                    mm(l[:, k, :], i + k, g, wrc, wrs, slice(0, E), g == 0, g == G - 1)
             S[i]["l"] = l
 
-        def U(i):
-            u = psum.tile([P, R], F32, name="u", bufs=NU)
+        def l(i):
+            logits(i, 1)
+
+        def L(i):
+            logits(i, 2)
+
+        def u(i):
+            t = psum.tile([P, R], F32, name="u", bufs=NU)
             for g in range(G):
-                mm(u[:], i, g, ac, as_, slice(0, R), g == 0, g == G - 1)
-            S[i]["u"] = u
+                mm(t[:], i, g, ac, as_, slice(0, R), g == 0, g == G - 1)
+            S[i]["u"] = t
+
+        def bias(i, n):
+            lb = work.tile([P, n, E], F32, name="lb%d" % n, align_bytes=64)
+            nc.vector.tensor_tensor(
+                out=lb[:], in0=S[i]["l"][:], in1=brb[:].unsqueeze(1).to_broadcast([P, n, E]), op=ALU.add
+            )
+            for k in range(n):
+                S[i + k]["lb"] = lb[:, k, :]
+            S[i]["lbs"] = lb
+
+        def a(i):
+            bias(i, 1)
 
         def A(i):
-            lb = work.tile([P, E], F32, name="lb", align_bytes=64)
-            nc.vector.tensor_tensor(out=lb[:], in0=S[i]["l"][:], in1=brb[:], op=ALU.add)
-            S[i]["lb"] = lb
+            bias(i, 2)
+
+        def rowmax(i, n):
+            nm = work.tile([P, n], F32, name="nm%d" % n, align_bytes=64)
+            sm = work.tile([P, n], F32, name="sm%d" % n, align_bytes=64)
+            nc.vector.tensor_reduce(out=nm[:], in_=S[i]["lbs"][:], axis=AX.X, op=ALU.max, negate=True)
+            for k in range(n):
+                S[i + k]["nm"], S[i + k]["sm"] = nm[:, k : k + 1], sm[:, k : k + 1]
+            S[i]["sms"] = sm
+
+        def a2(i):
+            rowmax(i, 1)
 
         def A2(i):
-            nm = work.tile([P, 1], F32, name="nm", align_bytes=64)
-            nc.vector.tensor_reduce(out=nm[:], in_=S[i]["lb"][:], axis=AX.X, op=ALU.max, negate=True)
-            S[i]["nm"] = nm
+            rowmax(i, 2)
 
-        def X(i):
+        def x(i):
             ex = work.tile([P, E], F32, name="ex", align_bytes=64)
-            sm = work.tile([P, 1], F32, name="sm", align_bytes=64)
-            nc.scalar.activation(out=ex[:], in_=S[i]["lb"][:], func=ACTF.Exp, bias=S[i]["nm"][:], scale=1.0, accum_out=sm[:])
-            S[i]["ex"], S[i]["sm"] = ex, sm
+            nc.scalar.activation(
+                out=ex[:], in_=S[i]["lb"], func=ACTF.Exp, bias=S[i]["nm"], scale=1.0, accum_out=S[i]["sm"]
+            )
+            S[i]["ex"] = ex
 
-        def R1(i):
-            r0 = work.tile([P, 1], F32, name="r0", align_bytes=64)
-            nc.vector.reciprocal(out=r0[:], in_=S[i]["sm"][:])
+        def rec(i, n):
+            r0 = work.tile([P, n], F32, name="r0%d" % n, align_bytes=64)
+            nc.vector.reciprocal(out=r0[:], in_=S[i]["sms"][:])
             S[i]["r0"] = r0
+            for k in range(n):
+                S[i + k]["r"] = r0[:, k : k + 1]
+
+        def r(i):
+            rec(i, 1)
+
+        def RC(i):
+            rec(i, 2)
+
+        def times(i, n):
+            r1 = work.tile([P, n], F32, name="r1%d" % n, align_bytes=64)
+            nc.vector.tensor_scalar(out=r1[:], in0=S[i]["r0"][:], scalar1=float(E), scalar2=None, op0=ALU.mult)
+            for k in range(n):
+                S[i + k]["r"] = r1[:, k : k + 1]
+
+        def r2(i):
+            times(i, 1)
 
         def R2(i):
-            r1 = work.tile([P, 1], F32, name="r1", align_bytes=64)
-            nc.vector.tensor_scalar(out=r1[:], in0=S[i]["r0"][:], scalar1=float(E), scalar2=None, op0=ALU.mult)
-            S[i]["r"] = r1
+            times(i, 2)
 
-        def Z(i, u):
-            if u == 0:
-                S[i]["z"] = work.tile([P, 2, E, 2], BF16, name="z", align_bytes=64)
+        def newz(i):
+            j = i if i < NS else i - i % 2
+            if "z" not in S[j]:
+                n = 1 if i < NS else 2
+                S[j]["z"] = work.tile([P, n, R], BF16, name="z%d" % n, align_bytes=64)
+            return S[j]["z"][:, i - j, :]
+
+        def n(i):
+            gt = work.tile([P, E], F32, name="gt", align_bytes=64)
+            nc.vector.tensor_scalar(
+                out=gt[:], in0=S[i]["ex"][:], scalar1=S[i]["r"], scalar2=float(E), op0=ALU.mult, op1=ALU.mult
+            )
+            S[i]["gt"] = gt
+
+        def z(i):
+            nc.vector.tensor_tensor(
+                out=newz(i).rearrange("p (u m e) -> p u m e", u=2, e=2),
+                in0=S[i]["u"][:].rearrange("p (m u e) -> p u m e", u=2, e=2),
+                in1=S[i]["gt"][:].unsqueeze(1).unsqueeze(3).to_broadcast([P, 2, E, 2]),
+                op=ALU.mult,
+            )
+
+        def zh(i, h):
             nc.vector.scalar_tensor_tensor(
-                out=S[i]["z"][:, u, :, :],
-                in0=S[i]["u"][:].rearrange("p (m u e) -> p u m e", u=2, e=2)[:, u, :, :],
-                scalar=S[i]["r"][:],
+                out=newz(i).rearrange("p (u m e) -> p u m e", u=2, e=2)[:, h, :, :],
+                in0=S[i]["u"][:].rearrange("p (m u e) -> p u m e", u=2, e=2)[:, h, :, :],
+                scalar=S[i]["r"],
                 in1=S[i]["ex"][:].unsqueeze(2).to_broadcast([P, E, 2]),
                 op0=ALU.mult,
                 op1=ALU.mult,
             )
 
-        def ZT(i):
-            t = psum.tile([P, 2, P], F32, name="lz", bufs=NLZ)
-            words = S[i]["z"][:].rearrange("p u m e -> p (u m e)").bitcast(F32)
-            for u in range(2):
-                nc.tensor.transpose(t[:, u, :], words[:, P * u : P * (u + 1)], ident[:])
+        def turnz(i, n):
+            t = psum.tile([P, n, 2, P], F32, name="lz", bufs=NLZ)
+            for k in range(n):
+                words = S[i]["z"][:, k, :].bitcast(F32)
+                for h in range(2):
+                    nc.tensor.transpose(t[:, k, h, :], words[:, P * h : P * (h + 1)] if ZPERM else words[:, h:256:2], ident[:])
             S[i]["zt"] = t
 
-        def ZE(i):
-            t = work.tile([P, P, 4], BF16, name="zg", align_bytes=64)
+        def zt(i):
+            turnz(i, 1)
+
+        def ZT(i):
+            turnz(i, 2)
+
+        def emptyz(i, n):
+            t = work.tile([P, n, P, 4], BF16, name="zg%d" % n, align_bytes=64)
             nc.scalar.copy(
-                out=t[:].rearrange("p n t -> p (n t)").bitcast(F32).rearrange("p (n u) -> p n u", u=2),
-                in_=S[i]["zt"][:].rearrange("p u n -> p n u"),
+                out=t[:].rearrange("p k n t -> p (k n t)").bitcast(F32).rearrange("p (k n u) -> p k n u", k=n, u=2),
+                in_=S[i]["zt"][:].rearrange("p k u n -> p k n u"),
             )
             S[i]["zg"] = t
 
+        def ze(i):
+            emptyz(i, 1)
+
+        def ZE(i):
+            emptyz(i, 2)
+
+        def quantz(i, n):
+            c = work.tile([P, n, P], U32, name="zc%d" % n, align_bytes=64)
+            s = work.tile([P, n, P], U8, name="zcs%d" % n, align_bytes=64)
+            nc.vector.quantize_mx(
+                out=c[:].rearrange("p k n -> p (k n)").bitcast(FP8X4),
+                scales=s[:].rearrange("p k n -> p (k n)"),
+                in_=S[i]["zg"][:].rearrange("p k n t -> p (k n t)"),
+            )
+            for k in range(n):
+                S[i + k]["zc"], S[i + k]["zcs"] = c[:, k, :], s[:, k, :]
+
+        def zq(i):
+            quantz(i, 1)
+
         def ZQ(i):
-            c = work.tile([P, P], U32, name="zc", align_bytes=64)
-            s = work.tile([P, P], U8, name="zcs", align_bytes=64)
-            nc.vector.quantize_mx(out=c[:].bitcast(FP8X4), scales=s[:], in_=S[i]["zg"][:].rearrange("p n t -> p (n t)"))
-            S[i]["zc"], S[i]["zcs"] = c, s
+            quantz(i, 2)
 
         def B(i, h):
             o = psum.tile([P, 512], F32, name="o", bufs=NO)
@@ -239,213 +359,209 @@ def tile_rankwisemoloradenserouter_w8_kernel(
             cols = slice(512 * h, 512 * h + 512)
             nc.tensor.matmul_mx(
                 out=S[i]["o%d" % h][:],
-                lhsT=S[i]["zc"][:].bitcast(FP8X4),
-                lhsT_scale=S[i]["zcs"][:],
+                lhsT=S[i]["zc"].bitcast(FP8X4),
+                lhsT_scale=S[i]["zcs"],
                 rhs=bc[:, cols].bitcast(FP8X4),
                 rhs_scale=bs[:, cols],
                 start=False,
                 stop=True,
             )
 
-        def EV(i, h):
-            t = work.tile([P, 512], F32, name="ot", bufs=4, align_bytes=64)
-            if i == NT - 1 and h == 1:
-                nc.vector.tensor_copy(out=t[:], in_=S[i]["o%d" % h][:])
-            else:
-                nc.scalar.copy(out=t[:], in_=S[i]["o%d" % h][:])
-            nc.sync.dma_start(out=ov[:, i, 512 * h : 512 * h + 512], in_=t[:])
+        def EV(i, h, v=False):
+            n = 2 if v else 1
+            for k in range(n):
+                c = 512 // n
+                t = work.tile([P, c], F32, name="ot%d" % n, bufs=4, align_bytes=64)
+                src = S[i]["o%d" % h][:, k * c : (k + 1) * c]
+                if k == 1:
+                    nc.vector.tensor_copy(out=t[:], in_=src)
+                else:
+                    nc.scalar.copy(out=t[:], in_=src)
+                nc.sync.dma_start(out=ov[:, i, 512 * h + k * c : 512 * h + (k + 1) * c], in_=t[:])
 
         dummy(ND1)
-        WV(0)
-        W(0)
-        WV(1)
-        W(1)
-        TR(0)
-        W(2)
-        WV(2)
-        M(0, 0)
-        W(3)
-        WV(3)
-        Q(0)
-        TR(1)
-        M(0, 1)
-        M(1, 0)
-        TR(2)
-        QB(0)
-        W(4)
-        WV(4)
-        M(1, 1)
-        L(0)
-        W(5)
-        U(0)
-        WV(5)
-        M(2, 0)
-        W(6)
-        TR(3)
-        A(0)
-        WV(6)
-        Q(1)
-        W(7)
-        A2(0)
+        wv(0)
+        w(0)
+        wv(1)
+        w(1)
+        t(0)
+        wv(2)
+        w(2)
+        ma(0)
+        w(3)
+        q(0)
+        t(1)
+        wv(3)
+        mb(0)
+        ma(1)
+        t(2)
+        qb(0)
+        mb(1)
+        l(0)
+        u(0)
+        ma(2)
+        w(4)
+        wv(4)
+        t(3)
+        q(1)
+        w(5)
+        a(0)
+        mb(2)
+        w(6)
+        u(1)
+        wv(5)
+        a2(0)
+        l(1)
+        ma(3)
+        t(4)
+        x(0)
+        q(2)
+        w(7)
         B(0, 1)
-        M(2, 1)
-        WV(7)
-        X(0)
-        L(1)
-        M(3, 0)
-        U(1)
-        A(1)
-        R1(0)
-        Q(2)
-        TR(4)
-        A2(1)
-        R2(0)
-        M(3, 1)
-        L(2)
-        X(1)
-        B(1, 1)
-        Z(0, 0)
-        A(2)
-        R1(1)
-        TR(5)
-        Q(3)
-        Z(0, 1)
-        A2(2)
-        L(3)
-        R2(1)
-        M(4, 0)
-        U(2)
-        X(2)
-        Z(1, 0)
+        a(1)
+        wv(6)
+        r(0)
+        mb(3)
+        l(2)
         B(0, 0)
-        A(3)
-        R1(2)
-        M(4, 1)
-        ZT(0)
-        Z(1, 1)
-        ZE(0)
-        A2(3)
-        TR(6)
-        R2(2)
-        Q(4)
-        X(3)
-        Z(2, 0)
-        ZT(1)
-        ZQ(0)
-        U(3)
-        M(5, 0)
-        ZE(1)
+        n(0)
+        a2(1)
+        q(3)
+        t(5)
+        a(2)
+        wv(7)
+        x(1)
+        z(0)
+        l(3)
+        B(1, 1)
+        a2(2)
+        r(1)
+        a(3)
+        u(2)
+        n(1)
+        x(2)
+        ma(4)
+        zt(0)
+        a2(3)
+        z(1)
+        ze(0)
+        x(3)
+        r(2)
+        mb(4)
+        zt(1)
+        u(3)
+        zq(0)
+        n(2)
+        ze(1)
+        q(4)
         C(0, 0)
-        Z(2, 1)
-        L(4)
-        ZQ(1)
+        z(2)
         C(0, 1)
-        R1(3)
-        M(5, 1)
-        EV(0, 0)
-        U(4)
-        A(4)
+        l(4)
+        zq(1)
+        t(6)
+        r(3)
         EV(0, 1)
-        R2(3)
+        ma(5)
+        u(4)
+        EV(0, 0)
+        n(3)
+        a(4)
+        mb(5)
         C(1, 1)
-        M(6, 0)
-        TR(7)
-        Z(3, 0)
-        EV(1, 1)
-        A2(4)
-        ZT(2)
-        Q(5)
-        B(2, 1)
-        Z(3, 1)
-        ZE(2)
-        M(6, 1)
-        X(4)
+        zt(2)
+        a2(4)
         B(1, 0)
-        ZQ(2)
-        L(5)
-        R1(4)
-        M(7, 0)
+        z(3)
+        ze(2)
         C(1, 0)
-        U(5)
-        A(5)
+        x(4)
+        q(5)
+        EV(1, 1)
+        t(7)
+        zq(2)
+        r(4)
+        ma(6)
         EV(1, 0)
-        R2(4)
-        Q(6)
+        l(5)
+        u(5)
+        n(4)
+        a(5)
+        B(2, 1)
+        mb(6)
+        a2(5)
+        zt(3)
+        z(4)
         C(2, 1)
-        Z(4, 0)
-        ZT(3)
-        A2(5)
-        M(7, 1)
-        B(3, 1)
-        ZE(3)
-        X(5)
-        Z(4, 1)
         B(2, 0)
-        EV(2, 1)
-        Q(7)
-        L(6)
-        ZQ(3)
+        ze(3)
+        q(6)
+        x(5)
         C(2, 0)
-        R1(5)
-        U(6)
-        A(6)
-        R2(5)
+        ma(7)
+        EV(2, 1)
+        zt(4)
+        zq(3)
+        u(6)
+        r(5)
+        mb(7)
+        ze(4)
+        B(3, 1)
         EV(2, 0)
-        A2(6)
-        L(7)
-        Z(5, 0)
+        n(5)
+        zq(4)
+        l(6)
+        q(7)
         C(3, 1)
-        B(4, 1)
-        X(6)
-        A(7)
-        Z(5, 1)
-        EV(3, 1)
-        A2(7)
-        ZT(4)
-        R1(6)
-        U(7)
-        R2(6)
-        ZE(4)
-        X(7)
-        Z(6, 0)
         B(3, 0)
-        ZQ(4)
-        R1(7)
-        Z(6, 1)
-        ZT(5)
-        R2(7)
+        a(6)
+        z(5)
+        EV(3, 1)
         C(3, 0)
-        ZE(5)
-        C(4, 1)
-        Z(7, 0)
-        B(5, 1)
+        l(7)
+        a2(6)
+        B(4, 1)
+        a(7)
+        u(7)
+        x(6)
         EV(3, 0)
-        ZQ(5)
-        Z(7, 1)
-        EV(4, 1)
-        ZT(6)
-        C(5, 1)
-        ZE(6)
+        a2(7)
+        zt(5)
+        r(6)
+        C(4, 1)
+        n(6)
         B(4, 0)
-        EV(5, 1)
+        ze(5)
+        z(6)
+        x(7)
         C(4, 0)
-        ZQ(6)
-        ZT(7)
-        B(6, 1)
-        ZE(7)
+        EV(4, 1)
+        B(5, 1)
+        zq(5)
+        r(7)
         EV(4, 0)
-        C(6, 1)
+        zt(6)
+        n(7)
+        C(5, 1)
+        z(7)
         B(5, 0)
-        ZQ(7)
-        EV(6, 1)
+        ze(6)
+        EV(5, 1)
         C(5, 0)
-        B(7, 1)
+        zq(6)
+        B(6, 1)
         EV(5, 0)
-        C(7, 1)
+        zt(7)
+        C(6, 1)
         B(6, 0)
-        EV(7, 1)
+        ze(7)
+        EV(6, 1)
         C(6, 0)
-        B(7, 0)
+        zq(7)
+        B(7, 1)
         EV(6, 0)
+        C(7, 1)
+        B(7, 0)
+        EV(7, 1)
         C(7, 0)
-        EV(7, 0)
+        EV(7, 0, True)

from contextlib import ExitStack

import concourse.mybir as mybir
from concourse.masks import make_identity

T, D, F, E, R = 1024, 1024, 1024, 128, 512
P = 128
NT = T // P
G = D // 512
NXT, NLZ, NU, NO, NWORK, ND1, ND2, ZPERM, WG, NS = 2, 1, 2, 3, 8, 3, 2, True, True, 8

FLOPS = 2 * T * D * (F + E + R) + 2 * T * R * F

F32 = mybir.dt.float32
BF16 = mybir.dt.bfloat16
I32 = mybir.dt.int32
U32 = mybir.dt.uint32
U8 = mybir.dt.uint8
FP8 = mybir.dt.float8_e4m3fn
FP8X4 = mybir.dt.float8_e4m3fn_x4
ALU = mybir.AluOpType
ACTF = mybir.ActivationFunctionType
AX = mybir.AxisListType


def tile_rankwisemoloradenserouter_w8_kernel(
    tc, x_bytes, x_scale, w0_words, w0_scales, wr_words, wr_scales, br, a_words, a_scales, b_words, b_scales, out
):
    nc = tc.nc
    with ExitStack() as ctx:
        keep = ctx.enter_context(tc.tile_pool(name="keep", bufs=1))
        work = ctx.enter_context(tc.tile_pool(name="work", bufs=NWORK))
        psum = ctx.enter_context(tc.psum_pool(name="psum", bufs=1))
        ctx.enter_context(tc.manual_schedule())

        ident = keep.tile([P, P], F32, name="ident", align_bytes=64)
        xb = keep.tile([P, NT, D], U8, name="xb", align_bytes=64)
        xs = keep.tile([P, G, 4], F32, name="xs", align_bytes=64)
        brb = keep.tile([P, E], BF16, name="brb", align_bytes=64)
        w0c = keep.tile([P, G, F], U32, name="w0c", align_bytes=64)
        wrc = keep.tile([P, G, E], U32, name="wrc", align_bytes=64)
        ac = keep.tile([P, G, R], U32, name="ac", align_bytes=64)
        bc = keep.tile([P, F], U32, name="bc", align_bytes=64)
        w0s = keep.tile([P, F], U8, name="w0s", align_bytes=64)
        wrs = keep.tile([P, E], U8, name="wrs", align_bytes=64)
        as_ = keep.tile([P, R], U8, name="as_", align_bytes=64)
        bs = keep.tile([P, F], U8, name="bs", align_bytes=64)
        warm = keep.tile([P, 1], F32, name="warm", align_bytes=64)
        dmy = keep.tile([P, 512], BF16, name="dmy", align_bytes=64)

        xv = x_bytes.rearrange("(p i) k -> p i k", i=NT)
        ov = out.rearrange("(p i) f -> p i f", i=NT)

        def load_words(dst, src):
            nc.sync.dma_start(out=dst.bitcast(I32), in_=src.bitcast(I32))

        def load_scales(dst, src, g):
            for q in range(4):
                nc.sync.dma_start(
                    out=dst[32 * q : 32 * q + 4 * g, :].bitcast(I32),
                    in_=src[:, 4 * q : 4 * q + 4, :].bitcast(I32),
                )

        nc.vector.memset(wrs[:].bitcast(I32), 0)
        nc.vector.memset(as_[:].bitcast(I32), 0)
        nc.vector.memset(w0s[:].bitcast(I32), 0)
        nc.vector.memset(dmy[:].bitcast(I32), 0)
        nc.vector.memset(warm[:], 0.0)
        nc.vector.memset(bs[:].bitcast(I32), 0)
        make_identity(nc, ident[:])

        nc.sync.dma_start(out=xb[:, 0, :], in_=xv[:, 0, :])
        nc.scalar.dma_start(out=xs[:], in_=x_scale.rearrange("o (g p t) -> p (o g) t", p=P, t=4))
        nc.scalar.activation(out=warm[:], in_=warm[:], func=ACTF.Exp)
        nc.sync.dma_start(out=xb[:, 1, :], in_=xv[:, 1, :])
        nc.sync.dma_start(out=xb[:, 2:4, :], in_=xv[:, 2:4, :])
        load_words(wrc[:], wr_words.rearrange("g p n t -> p g (n t)"))
        load_scales(wrs, wr_scales, G)
        load_words(ac[:], a_words.rearrange("g p n t -> p g (n t)"))
        load_scales(as_, a_scales, G)
        nc.sync.dma_start(out=brb[:], in_=br.partition_broadcast(P))
        nc.sync.dma_start(out=xb[:, 4:8, :], in_=xv[:, 4:8, :])
        load_words(w0c[:], w0_words.rearrange("g p n t -> p g (n t)"))
        load_scales(w0s, w0_scales, G)
        load_words(bc[:], b_words.rearrange("g p n t -> p g (n t)")[:, 0, :])
        load_scales(bs, b_scales, 1)

        S = [dict() for i in range(NT)]

        def dummy(n):
            for k in range(n):
                t = psum.tile([P, 512], F32, name="u", bufs=NU)
                nc.tensor.matmul(t[:], lhsT=dmy[:, 0:P], rhs=dmy[:], start=True, stop=True)

        def fp8(i, k0, k1):
            return xb[:, i, k0:k1].bitcast(FP8)

        def newx(i):
            if "xw" not in S[i]:
                S[i]["xw"] = work.tile([P, D], BF16, name="xw", align_bytes=64)
            return S[i]["xw"]

        def wv(i):
            if i < 2:
                nc.vector.tensor_copy(out=newx(i)[:, 0:512], in_=fp8(i, 0, 512))
            elif WG:
                for k in (0, 256):
                    nc.gpsimd.tensor_copy(out=newx(i)[:, k : k + 256], in_=fp8(i, k, k + 256))

        def w(i):
            k = 512 if i < 2 or WG else 0
            nc.scalar.copy(out=newx(i)[:, k:D], in_=fp8(i, k, D))

        def Wa(i):
            nc.scalar.copy(out=newx(i)[:], in_=fp8(i, 0, D))

        def Wb(i):
            for k in range(4):
                nc.gpsimd.tensor_copy(out=newx(i + 1)[:, 256 * k : 256 * (k + 1)], in_=fp8(i + 1, 256 * k, 256 * (k + 1)))

        def turn(dst, i, g):
            words = S[i]["xw"][:].bitcast(F32)
            for u in range(2):
                nc.tensor.transpose(dst[u], words[:, 256 * g + u : 256 * (g + 1) : 2], ident[:])

        def t(i):
            if i == 0:
                S[i]["xt"] = [psum.tile([P, 2, P], F32, name="xt", bufs=NXT)[:, :, :] for g in range(G)]
            else:
                x1 = psum.tile([P, G, 2, P], F32, name="xt", bufs=NXT)
                S[i]["xt"] = [x1[:, g, :, :] for g in range(G)]
            for g in range(G):
                turn([S[i]["xt"][g][:, u, :] for u in range(2)], i, g)
            if i == 0:
                dummy(ND2)

        def T(i, g):
            xp = psum.tile([P, 2, 2, P], F32, name="xt", bufs=NXT)
            for k in range(2):
                turn([xp[:, u, k, :] for u in range(2)], i + k, g)
            S[i]["xt%d" % g] = xp[:].rearrange("p u k n -> p u (k n)")

        def scale(i, g, n, src):
            if "xg" not in S[i]:
                S[i]["xg"] = work.tile([P, G, n * P, 4], BF16, name="xg%d" % n, align_bytes=64)
            nc.vector.tensor_tensor(
                out=S[i]["xg"][:, g, :, :].rearrange("p n (u e) -> p n u e", e=2),
                in0=src.rearrange("p u n -> p (u n)").bitcast(BF16).rearrange("p (u n e) -> p n u e", u=2, e=2),
                in1=xs[:, g, :].rearrange("p (u e) -> p u e", e=2).unsqueeze(1).to_broadcast([P, n * P, 2, 2]),
                op=ALU.mult,
            )

        def ma(i):
            scale(i, 0, 1, S[i]["xt"][0])

        def mb(i):
            scale(i, 1, 1, S[i]["xt"][1])

        def M(i, g):
            scale(i, g, 2, S[i]["xt%d" % g])

        def quant(i, n, gs):
            if "xc" not in S[i]:
                S[i]["xc"] = keep.tile([P, G, n * P], U32, name="xc%d" % i, align_bytes=64)
                S[i]["xcs"] = keep.tile([P, G, n * P], U8, name="xcs%d" % i, align_bytes=64)
                for k in range(n):
                    S[i + k]["x"] = (S[i]["xc"], S[i]["xcs"], slice(k * P, (k + 1) * P))
            nc.vector.quantize_mx(
                out=S[i]["xc"][:, gs, :].rearrange("p g n -> p (g n)").bitcast(FP8X4),
                scales=S[i]["xcs"][:, gs, :].rearrange("p g n -> p (g n)"),
                in_=S[i]["xg"][:, gs, :, :].rearrange("p g n t -> p (g n t)"),
            )

        def q(i):
            quant(i, 1, slice(0, 1) if i == 0 else slice(0, G))

        def qb(i):
            quant(i, 1, slice(1, G))

        def Q(i):
            quant(i, 2, slice(0, G))

        def mm(dst, i, g, wc, ws, cols, start, stop):
            c, s, tok = S[i]["x"]
            nc.tensor.matmul_mx(
                out=dst,
                lhsT=c[:, g, tok].bitcast(FP8X4),
                lhsT_scale=s[:, g, tok],
                rhs=wc[:, g, cols].bitcast(FP8X4),
                rhs_scale=ws[4 * g : P, cols],
                start=start,
                stop=stop,
            )

        def logits(i, n):
            l = psum.tile([P, n, E], F32, name="lz", bufs=NLZ)
            for k in range(n):
                for g in range(G):
                    mm(l[:, k, :], i + k, g, wrc, wrs, slice(0, E), g == 0, g == G - 1)
            S[i]["l"] = l

        def l(i):
            logits(i, 1)

        def L(i):
            logits(i, 2)

        def u(i):
            t = psum.tile([P, R], F32, name="u", bufs=NU)
            for g in range(G):
                mm(t[:], i, g, ac, as_, slice(0, R), g == 0, g == G - 1)
            S[i]["u"] = t

        def bias(i, n):
            lb = work.tile([P, n, E], F32, name="lb%d" % n, align_bytes=64)
            nc.vector.tensor_tensor(
                out=lb[:], in0=S[i]["l"][:], in1=brb[:].unsqueeze(1).to_broadcast([P, n, E]), op=ALU.add
            )
            for k in range(n):
                S[i + k]["lb"] = lb[:, k, :]
            S[i]["lbs"] = lb

        def a(i):
            bias(i, 1)

        def A(i):
            bias(i, 2)

        def rowmax(i, n):
            nm = work.tile([P, n], F32, name="nm%d" % n, align_bytes=64)
            sm = work.tile([P, n], F32, name="sm%d" % n, align_bytes=64)
            nc.vector.tensor_reduce(out=nm[:], in_=S[i]["lbs"][:], axis=AX.X, op=ALU.max, negate=True)
            for k in range(n):
                S[i + k]["nm"], S[i + k]["sm"] = nm[:, k : k + 1], sm[:, k : k + 1]
            S[i]["sms"] = sm

        def a2(i):
            rowmax(i, 1)

        def A2(i):
            rowmax(i, 2)

        def x(i):
            ex = work.tile([P, E], F32, name="ex", align_bytes=64)
            nc.scalar.activation(
                out=ex[:], in_=S[i]["lb"], func=ACTF.Exp, bias=S[i]["nm"], scale=1.0, accum_out=S[i]["sm"]
            )
            S[i]["ex"] = ex

        def rec(i, n):
            r0 = work.tile([P, n], F32, name="r0%d" % n, align_bytes=64)
            nc.vector.reciprocal(out=r0[:], in_=S[i]["sms"][:])
            S[i]["r0"] = r0
            for k in range(n):
                S[i + k]["r"] = r0[:, k : k + 1]

        def r(i):
            rec(i, 1)

        def RC(i):
            rec(i, 2)

        def times(i, n):
            r1 = work.tile([P, n], F32, name="r1%d" % n, align_bytes=64)
            nc.vector.tensor_scalar(out=r1[:], in0=S[i]["r0"][:], scalar1=float(E), scalar2=None, op0=ALU.mult)
            for k in range(n):
                S[i + k]["r"] = r1[:, k : k + 1]

        def r2(i):
            times(i, 1)

        def R2(i):
            times(i, 2)

        def newz(i):
            j = i if i < NS else i - i % 2
            if "z" not in S[j]:
                n = 1 if i < NS else 2
                S[j]["z"] = work.tile([P, n, R], BF16, name="z%d" % n, align_bytes=64)
            return S[j]["z"][:, i - j, :]

        def n(i):
            gt = work.tile([P, E], F32, name="gt", align_bytes=64)
            nc.vector.tensor_scalar(
                out=gt[:], in0=S[i]["ex"][:], scalar1=S[i]["r"], scalar2=float(E), op0=ALU.mult, op1=ALU.mult
            )
            S[i]["gt"] = gt

        def z(i):
            nc.vector.tensor_tensor(
                out=newz(i).rearrange("p (u m e) -> p u m e", u=2, e=2),
                in0=S[i]["u"][:].rearrange("p (m u e) -> p u m e", u=2, e=2),
                in1=S[i]["gt"][:].unsqueeze(1).unsqueeze(3).to_broadcast([P, 2, E, 2]),
                op=ALU.mult,
            )

        def zh(i, h):
            nc.vector.scalar_tensor_tensor(
                out=newz(i).rearrange("p (u m e) -> p u m e", u=2, e=2)[:, h, :, :],
                in0=S[i]["u"][:].rearrange("p (m u e) -> p u m e", u=2, e=2)[:, h, :, :],
                scalar=S[i]["r"],
                in1=S[i]["ex"][:].unsqueeze(2).to_broadcast([P, E, 2]),
                op0=ALU.mult,
                op1=ALU.mult,
            )

        def turnz(i, n):
            t = psum.tile([P, n, 2, P], F32, name="lz", bufs=NLZ)
            for k in range(n):
                words = S[i]["z"][:, k, :].bitcast(F32)
                for h in range(2):
                    nc.tensor.transpose(t[:, k, h, :], words[:, P * h : P * (h + 1)] if ZPERM else words[:, h:256:2], ident[:])
            S[i]["zt"] = t

        def zt(i):
            turnz(i, 1)

        def ZT(i):
            turnz(i, 2)

        def emptyz(i, n):
            t = work.tile([P, n, P, 4], BF16, name="zg%d" % n, align_bytes=64)
            nc.scalar.copy(
                out=t[:].rearrange("p k n t -> p (k n t)").bitcast(F32).rearrange("p (k n u) -> p k n u", k=n, u=2),
                in_=S[i]["zt"][:].rearrange("p k u n -> p k n u"),
            )
            S[i]["zg"] = t

        def ze(i):
            emptyz(i, 1)

        def ZE(i):
            emptyz(i, 2)

        def quantz(i, n):
            c = work.tile([P, n, P], U32, name="zc%d" % n, align_bytes=64)
            s = work.tile([P, n, P], U8, name="zcs%d" % n, align_bytes=64)
            nc.vector.quantize_mx(
                out=c[:].rearrange("p k n -> p (k n)").bitcast(FP8X4),
                scales=s[:].rearrange("p k n -> p (k n)"),
                in_=S[i]["zg"][:].rearrange("p k n t -> p (k n t)"),
            )
            for k in range(n):
                S[i + k]["zc"], S[i + k]["zcs"] = c[:, k, :], s[:, k, :]

        def zq(i):
            quantz(i, 1)

        def ZQ(i):
            quantz(i, 2)

        def B(i, h):
            o = psum.tile([P, 512], F32, name="o", bufs=NO)
            for g in range(G):
                mm(o[:], i, g, w0c, w0s, slice(512 * h, 512 * h + 512), g == 0, False)
            S[i]["o%d" % h] = o

        def C(i, h):
            cols = slice(512 * h, 512 * h + 512)
            nc.tensor.matmul_mx(
                out=S[i]["o%d" % h][:],
                lhsT=S[i]["zc"].bitcast(FP8X4),
                lhsT_scale=S[i]["zcs"],
                rhs=bc[:, cols].bitcast(FP8X4),
                rhs_scale=bs[:, cols],
                start=False,
                stop=True,
            )

        def EV(i, h, v=False):
            n = 2 if v else 1
            for k in range(n):
                c = 512 // n
                t = work.tile([P, c], F32, name="ot%d" % n, bufs=4, align_bytes=64)
                src = S[i]["o%d" % h][:, k * c : (k + 1) * c]
                if k == 1:
                    nc.vector.tensor_copy(out=t[:], in_=src)
                else:
                    nc.scalar.copy(out=t[:], in_=src)
                nc.sync.dma_start(out=ov[:, i, 512 * h + k * c : 512 * h + (k + 1) * c], in_=t[:])

        dummy(ND1)
        wv(0)
        w(0)
        wv(1)
        w(1)
        t(0)
        wv(2)
        w(2)
        ma(0)
        w(3)
        q(0)
        t(1)
        wv(3)
        mb(0)
        ma(1)
        t(2)
        qb(0)
        mb(1)
        l(0)
        u(0)
        ma(2)
        w(4)
        wv(4)
        t(3)
        q(1)
        w(5)
        a(0)
        mb(2)
        w(6)
        u(1)
        wv(5)
        a2(0)
        l(1)
        ma(3)
        t(4)
        x(0)
        q(2)
        w(7)
        B(0, 1)
        a(1)
        wv(6)
        r(0)
        mb(3)
        l(2)
        B(0, 0)
        n(0)
        a2(1)
        q(3)
        t(5)
        a(2)
        wv(7)
        x(1)
        z(0)
        l(3)
        B(1, 1)
        a2(2)
        r(1)
        a(3)
        u(2)
        n(1)
        x(2)
        ma(4)
        zt(0)
        a2(3)
        z(1)
        ze(0)
        x(3)
        r(2)
        mb(4)
        zt(1)
        u(3)
        zq(0)
        n(2)
        ze(1)
        q(4)
        C(0, 0)
        z(2)
        C(0, 1)
        l(4)
        zq(1)
        t(6)
        r(3)
        EV(0, 1)
        ma(5)
        u(4)
        EV(0, 0)
        n(3)
        a(4)
        mb(5)
        C(1, 1)
        zt(2)
        a2(4)
        B(1, 0)
        z(3)
        ze(2)
        C(1, 0)
        x(4)
        q(5)
        EV(1, 1)
        t(7)
        zq(2)
        r(4)
        ma(6)
        EV(1, 0)
        l(5)
        u(5)
        n(4)
        a(5)
        B(2, 1)
        mb(6)
        a2(5)
        zt(3)
        z(4)
        C(2, 1)
        B(2, 0)
        ze(3)
        q(6)
        x(5)
        C(2, 0)
        ma(7)
        EV(2, 1)
        zt(4)
        zq(3)
        u(6)
        r(5)
        mb(7)
        ze(4)
        B(3, 1)
        EV(2, 0)
        n(5)
        zq(4)
        l(6)
        q(7)
        C(3, 1)
        B(3, 0)
        a(6)
        z(5)
        EV(3, 1)
        C(3, 0)
        l(7)
        a2(6)
        B(4, 1)
        a(7)
        u(7)
        x(6)
        EV(3, 0)
        a2(7)
        zt(5)
        r(6)
        C(4, 1)
        n(6)
        B(4, 0)
        ze(5)
        z(6)
        x(7)
        C(4, 0)
        EV(4, 1)
        B(5, 1)
        zq(5)
        r(7)
        EV(4, 0)
        zt(6)
        n(7)
        C(5, 1)
        z(7)
        B(5, 0)
        ze(6)
        EV(5, 1)
        C(5, 0)
        zq(6)
        B(6, 1)
        EV(5, 0)
        zt(7)
        C(6, 1)
        B(6, 0)
        ze(7)
        EV(6, 1)
        C(6, 0)
        zq(7)
        B(7, 1)
        EV(6, 0)
        C(7, 1)
        B(7, 0)
        EV(7, 1)
        C(7, 0)
        EV(7, 0, True)
